import numpy as np, ml_dtypes
CORES = [30,158,46,174,86,214]
N = 6
import mx_ref
NC, G = 192, 4
C = np.float32(0.019)
BF = ml_dtypes.bfloat16
def cut(t, i, w=512):
    return t[:, w * i:w * i + w]
def tile(rs):
    return np.stack(rs, axis=2).reshape(128, -1).astype(BF)
def layer(w, X):
    out = []
    for i in range(G):
        for t in range(len(X)):
            p = mx_ref.matmul(mx_ref.quantize(cut(w, len(X) * i + t)), X[t])
            z = p if t == 0 else z + p
        out.append(z)
    return out
def act(Z):
    return [np.maximum(z, 0) * C for z in Z]
def setup_inputs(rng):
    def f(*shape):
        return mx_ref.flush((rng.standard_normal(shape, dtype=np.float32) * np.exp2(rng.integers(-2, 3, shape[:-1] + (1,)))).astype(BF))
    return {"x": f(N, 128, 4 * NC), "w1": f(N, 128, G * 512), "w2": f(N, 128, 512)}
def setup_inputs_blocks(rng):
    d = setup_inputs(rng)
    for k in ("x", "w1", "w2"): d[k] = mx_ref.spread(d[k], rng, 2)
    return d
def setup_inputs_wide(rng):
    d = setup_inputs(rng)
    for k in ("x", "w1", "w2"): d[k] = mx_ref.flush((d[k].astype(np.float32) * np.exp2(rng.integers(-6, 7, (N, 1, 1))).astype(np.float32)).astype(BF))
    return d
def reference(x, w1, w2):
    X = [mx_ref.quantize(x[j]) for j in range(N)]
    y = np.zeros((N, 128, NC), np.float32)
    for c in range(N):
        for r in range(N):
            p = mx_ref.matmul(mx_ref.quantize(w2[r]), mx_ref.quantize(tile(act(layer(w1[r], [X[c]])))))
            y[c] = p if r == 0 else y[c] + p
    return {"y": y}

@@ -1,0 +1,197 @@
+from concourse.bass import DstId, RemoteDMATransfer
+from concourse.mybir import dt, AluOpType, ActivationFunctionType
+
+N, NC, SIM_CORES = 6, 192, 256
+SCALE = 0.019
+DIRECT = [1, 2]
+VIA = [[3, 5], [4]]
+
+SCRATCH = {
+    "xb": ("sbuf", [128, 4 * NC], "bfloat16"),
+    "w1b": ("sbuf", [128, 2048], "bfloat16"),
+    "w2b": ("sbuf", [128, 512], "bfloat16"),
+    "xq": ("sbuf", [128, NC], "float8_e4m3fn_x4"),
+    "xs": ("sbuf", [128, NC], "uint8"),
+    "w1q": ("sbuf", [128, 512], "float8_e4m3fn_x4"),
+    "w1s": ("sbuf", [128, 512], "uint8"),
+    "w2q": ("sbuf", [128, 128], "float8_e4m3fn_x4"),
+    "w2s": ("sbuf", [128, 128], "uint8"),
+    "rq": ("sbuf", [128, NC * (N - 1)], "float8_e4m3fn_x4"),
+    "rs": ("sbuf", [128, NC * (N - 1)], "uint8"),
+    "h": ("sbuf", [128, 4 * NC], "bfloat16"),
+    "hq": ("sbuf", [128, 2 * NC], "float8_e4m3fn_x4"),
+    "hs": ("sbuf", [128, 2 * NC], "uint8"),
+    "ys": ("sbuf", [128, NC * (N - 1)], "float32"),
+    "yl": ("sbuf", [128, NC * (N - 1)], "float32"),
+    "acc": ("sbuf", [128, NC], "float32"),
+    "pz": ("psum", [128, 2048], "float32"),
+    "po": ("psum", [128, 512], "float32"),
+    "py": ("psum", [128, 1024], "float32"),
+}
+SEMAPHORES = (["ldx", "ldw1a", "ldw1b", "ldw2", "xd", "wd", "zc", "asc", "avc", "hd", "my", "yc", "ad", "st", "sent", "hc", "hp"]
+              + ["x%d" % k for k in range(1, N)] + ["y%d" % k for k in range(1, N)])
+
+
+def count(mask):
+    return bin(mask).count("1")
+
+
+def same_chip(topo, a, b):
+    return topo.host(a) == topo.host(b) and topo.chip(a) == topo.chip(b)
+
+
+def helpers_of(rank, T, topo):
+    home = T.cores[rank]
+    found = []
+    for c in range(SIM_CORES):
+        if same_chip(topo, c, home) and topo.die(c) != topo.die(home):
+            if all(topo.may_write(c, d) for d in T.cores if d != home):
+                found.append(c)
+    return found[:len(VIA)]
+
+
+def dest(d, src, topo):
+    rid, pid = topo.addr(d, src)
+    return DstId(rid=rid, pnc=pid)
+
+
+def part(buf, k):
+    return buf[:, NC * (k - 1):NC * k]
+
+
+def rank_program(g, core, T, topo):
+    rank = T.rank_of(core)
+    if rank is None:
+        for r in range(N):
+            if same_chip(topo, core, T.cores[r]):
+                hs = helpers_of(r, T, topo)
+                if core in hs:
+                    helper(g, core, r, VIA[hs.index(core)], T, topo)
+        return
+
+    sem = T.sem
+    to = {k: T.cores[(rank + k) % N] for k in range(1, N)}
+    back = {k: T.cores[(rank - k) % N] for k in range(1, N)}
+    hs = helpers_of(rank, T, topo)
+
+    g.sync.dma_start(T.xb[:], T.x[:]).then_inc(sem.ldx, 16)
+    g.sync.dma_start(T.w1b[:, 0:1024], T.w1[:, 0:1024]).then_inc(sem.ldw1a, 16)
+    g.sync.dma_start(T.w1b[:, 1024:2048], T.w1[:, 1024:2048]).then_inc(sem.ldw1b, 16)
+    g.sync.dma_start(T.w2b[:], T.w2[:]).then_inc(sem.ldw2, 16)
+
+    sent = 0
+    g.wait_ge(sem.xd, 1)
+    for i in range(max(len(DIRECT), len(hs))):
+        for what in range(2):
+            transfers = []
+            if i < len(DIRECT):
+                k = DIRECT[i]
+                d = to[k]
+                m = topo.mask(core, d)
+                src, dst = ((T.xq[:].bitcast(dt.uint8), part(T.rq, k).bitcast(dt.uint8)) if what == 0
+                            else (T.xs[:], part(T.rs, k)))
+                transfers.append(RemoteDMATransfer(dst_ids=[dest(d, core, topo)], dma_engine_mask=m,
+                                                   remote_sem=sem["x%d" % k], src=src, dst=dst, alu_op=0))
+                sent += count(m)
+            if i < len(hs):
+                d = hs[i]
+                m = topo.mask(core, d) & ~topo.mask(core, to[1])
+                src, dst = ((T.xq[:].bitcast(dt.uint8), T.xq[:].bitcast(dt.uint8)) if what == 0
+                            else (T.xs[:], T.xs[:]))
+                transfers.append(RemoteDMATransfer(dst_ids=[dest(d, core, topo)], dma_engine_mask=m,
+                                                   remote_sem=sem.hc if what == 0 else sem.hp, src=src, dst=dst, alu_op=0))
+                sent += count(m)
+            g.remote_dma_fused(transfers, local_sem=sem.sent)
+    for k in range(1, N):
+        g.wait_ge(sem.yc, k)
+        d = back[k]
+        rid, pid = topo.addr(d, core)
+        m = topo.mask(core, d)
+        g.remote_dma(out_ap=part(T.yl, k), in_ap=part(T.ys, k), remote_sem=sem["y%d" % k], local_sem=sem.sent,
+                     pid=pid, routing_id=rid, dma_engine_mask=m)
+        sent += count(m)
+    g.wait_ge(sem.sent, sent)
+
+    for k in range(N):
+        if k == 0:
+            xq, xs = T.xq[:], T.xs[:]
+            g.tensor.wait_ge(sem.xd, 1)
+        else:
+            xq, xs = part(T.rq, k), part(T.rs, k)
+            src = back[k]
+            g.tensor.wait_ge(sem["x%d" % k], 2 * count(topo.mask(src, core)))
+        for i in range(4):
+            if k == 0 and i % 2 == 0:
+                g.tensor.wait_ge(sem.wd, i // 2 + 1)
+            g.tensor.matmul_mx(T.pz[:, 512 * i:512 * i + NC], T.w1q[:, 128 * i:128 * i + 128], T.w1s[:, 128 * i:128 * i + 128],
+                               xq, xs, True, True).then_inc(sem.zc, 1)
+        b = k % 2
+        if k == 0:
+            g.tensor.wait_ge(sem.wd, 3)
+        g.tensor.wait_ge(sem.hd, k + 1)
+        if k >= 3:
+            g.tensor.wait_ge(sem.yc, k - 2)
+        out = T.po[:, 0:NC] if k == 0 else T.py[:, 512 * b:512 * b + NC]
+        g.tensor.matmul_mx(out, T.w2q[:], T.w2s[:], T.hq[:, NC * b:NC * b + NC], T.hs[:, NC * b:NC * b + NC],
+                           True, True).then_inc(sem.my, 1)
+
+    for k in range(N):
+        for i in (0, 2):
+            g.scalar.wait_ge(sem.zc, 4 * k + i + 1)
+            g.scalar.activation(T.h[:, i:4 * NC:4], T.pz[:, 512 * i:512 * i + NC], ActivationFunctionType.Relu,
+                                scale=SCALE).then_inc(sem.asc, 1)
+        if k:
+            b = k % 2
+            g.scalar.wait_ge(sem.my, k + 1)
+            g.scalar.activation(part(T.ys, k), T.py[:, 512 * b:512 * b + NC], ActivationFunctionType.Copy).then_inc(sem.yc, 1)
+
+    g.vector.wait_ge(sem.ldx, 16)
+    g.vector.quantize_mx(T.xq[:], T.xs[:], T.xb[:]).then_inc(sem.xd, 1)
+    g.vector.wait_ge(sem.ldw1a, 16)
+    g.vector.quantize_mx(T.w1q[:, 0:256], T.w1s[:, 0:256], T.w1b[:, 0:1024]).then_inc(sem.wd, 1)
+    g.vector.wait_ge(sem.ldw1b, 16)
+    g.vector.quantize_mx(T.w1q[:, 256:512], T.w1s[:, 256:512], T.w1b[:, 1024:2048]).then_inc(sem.wd, 1)
+    for k in range(N):
+        b = k % 2
+        for i in (1, 3):
+            g.vector.wait_ge(sem.zc, 4 * k + i + 1)
+            g.vector.tensor_scalar(T.h[:, i:4 * NC:4], T.pz[:, 512 * i:512 * i + NC], 0.0, SCALE,
+                                   AluOpType.max, AluOpType.mult).then_inc(sem.avc, 1)
+        g.vector.wait_ge(sem.asc, 2 * k + 2)
+        g.vector.wait_ge(sem.avc, 2 * k + 2)
+        g.vector.quantize_mx(T.hq[:, NC * b:NC * b + NC], T.hs[:, NC * b:NC * b + NC], T.h[:]).then_inc(sem.hd, 1)
+        if k == 0:
+            g.vector.wait_ge(sem.ldw2, 16)
+            g.vector.quantize_mx(T.w2q[:], T.w2s[:], T.w2b[:]).then_inc(sem.wd, 1)
+    g.vector.wait_ge(sem.my, 1)
+    for k in range(1, N):
+        src = to[k]
+        g.vector.wait_ge(sem["y%d" % k], count(topo.mask(src, core)))
+        if k > 1:
+            g.vector.wait_ge(sem.ad, k - 1)
+        g.vector.tensor_tensor(T.acc[:], T.po[:, 0:NC] if k == 1 else T.acc[:], part(T.yl, k),
+                               AluOpType.add).then_inc(sem.ad, 1)
+
+    g.sync.wait_ge(sem.ad, N - 1)
+    g.sync.dma_start(T.y[:], T.acc[:]).then_inc(sem.st, 16)
+    g.sync.wait_ge(sem.st, 16)
+
+
+def helper(g, core, rank, rounds, T, topo):
+    sem = T.sem
+    inner = count(topo.mask(T.cores[rank], core) & ~topo.mask(T.cores[rank], T.cores[(rank + 1) % N]))
+    sent = 0
+    for n, k in enumerate(rounds):
+        d = T.cores[(rank + k) % N]
+        rid, pid = topo.addr(d, core)
+        m = topo.mask(core, d)
+        if n == 0:
+            g.wait_ge(sem.hc, inner)
+        g.remote_dma(out_ap=part(T.rq, k).bitcast(dt.uint8), in_ap=T.xq[:].bitcast(dt.uint8), remote_sem=sem["x%d" % k],
+                     local_sem=sem.sent, pid=pid, routing_id=rid, dma_engine_mask=m)
+        if n == 0:
+            g.wait_ge(sem.hp, inner)
+        g.remote_dma(out_ap=part(T.rs, k), in_ap=T.xs[:], remote_sem=sem["x%d" % k],
+                     local_sem=sem.sent, pid=pid, routing_id=rid, dma_engine_mask=m)
+        sent += 2 * count(m)
+    g.wait_ge(sem.sent, sent)

@@ -1,10 +1,14 @@
 from concourse.bass import DstId, RemoteDMATransfer
 from concourse.mybir import dt, AluOpType, ActivationFunctionType
 
-N, NC, SIM_CORES = 6, 192, 256
+N, NC, WC, SIM_CORES = 6, 192, 640, 256
 SCALE = 0.019
-DIRECT = [1, 2]
-VIA = [[3, 5], [4]]
+SHIFT = 3
+ROUNDS = [1, 2, 4, 5]
+PIECES = [(0, 256), (256, WC)]
+STEPS = [[("d", 1), ("x", 0)], [("d", 2)], [("w", 1, 0)], [("d", 4)], [("w", 0, 1)]]
+VIA = [[("x", 5), ("w", 1)], [("w", 0)]]
+AHEAD = [0, 0, 0, 3, 0]
 
 SCRATCH = {
     "xb": ("sbuf", [128, 4 * NC], "bfloat16"),
@@ -12,13 +16,13 @@ SCRATCH = {
     "w2b": ("sbuf", [128, 512], "bfloat16"),
     "xq": ("sbuf", [128, NC], "float8_e4m3fn_x4"),
     "xs": ("sbuf", [128, NC], "uint8"),
-    "w1q": ("sbuf", [128, 512], "float8_e4m3fn_x4"),
-    "w1s": ("sbuf", [128, 512], "uint8"),
-    "w2q": ("sbuf", [128, 128], "float8_e4m3fn_x4"),
-    "w2s": ("sbuf", [128, 128], "uint8"),
+    "wq": ("sbuf", [128, WC], "float8_e4m3fn_x4"),
+    "ws": ("sbuf", [128, WC], "uint8"),
+    "vq": ("sbuf", [128, WC], "float8_e4m3fn_x4"),
+    "vs": ("sbuf", [128, WC], "uint8"),
     "rq": ("sbuf", [128, NC * (N - 1)], "float8_e4m3fn_x4"),
     "rs": ("sbuf", [128, NC * (N - 1)], "uint8"),
-    "h": ("sbuf", [128, 4 * NC], "bfloat16"),
+    "h": ("sbuf", [128, 8 * NC], "bfloat16"),
     "hq": ("sbuf", [128, 2 * NC], "float8_e4m3fn_x4"),
     "hs": ("sbuf", [128, 2 * NC], "uint8"),
     "ys": ("sbuf", [128, NC * (N - 1)], "float32"),
@@ -28,8 +32,9 @@ SCRATCH = {
     "po": ("psum", [128, 512], "float32"),
     "py": ("psum", [128, 1024], "float32"),
 }
-SEMAPHORES = (["ldx", "ldw1a", "ldw1b", "ldw2", "xd", "wd", "zc", "asc", "avc", "hd", "my", "yc", "ad", "st", "sent", "hc", "hp"]
-              + ["x%d" % k for k in range(1, N)] + ["y%d" % k for k in range(1, N)])
+SEMAPHORES = (["ldx", "ldw1a", "ldw1b", "ldw2", "xd", "wd", "zc", "asc", "avc", "hd", "my", "yc", "ad", "st", "sent", "hxc", "hxs"]
+              + [s + "%d" % p for s in ("hwc", "hws", "v") for p in range(len(PIECES))]
+              + [s + "%d" % k for s in ("x", "y") for k in range(1, N)])
 
 
 def count(mask):
@@ -55,8 +60,17 @@ def dest(d, src, topo):
     return DstId(rid=rid, pnc=pid)
 
 
+def inner_mask(rank, h, T, topo):
+    home = T.cores[rank]
+    return topo.mask(home, h) & ~topo.mask(home, T.cores[(rank + 1) % N])
+
+
 def part(buf, k):
     return buf[:, NC * (k - 1):NC * k]
+
+
+def both(codes, planes, lo, hi):
+    return codes[:, lo:hi].bitcast(dt.uint8), planes[:, lo:hi]
 
 
 def rank_program(g, core, T, topo):
@@ -81,29 +95,32 @@ def rank_program(g, core, T, topo):
 
     sent = 0
     g.wait_ge(sem.xd, 1)
-    for i in range(max(len(DIRECT), len(hs))):
+    for step in STEPS:
         for what in range(2):
             transfers = []
-            if i < len(DIRECT):
-                k = DIRECT[i]
-                d = to[k]
-                m = topo.mask(core, d)
-                src, dst = ((T.xq[:].bitcast(dt.uint8), part(T.rq, k).bitcast(dt.uint8)) if what == 0
-                            else (T.xs[:], part(T.rs, k)))
-                transfers.append(RemoteDMATransfer(dst_ids=[dest(d, core, topo)], dma_engine_mask=m,
-                                                   remote_sem=sem["x%d" % k], src=src, dst=dst, alu_op=0))
-                sent += count(m)
-            if i < len(hs):
-                d = hs[i]
-                m = topo.mask(core, d) & ~topo.mask(core, to[1])
-                src, dst = ((T.xq[:].bitcast(dt.uint8), T.xq[:].bitcast(dt.uint8)) if what == 0
-                            else (T.xs[:], T.xs[:]))
-                transfers.append(RemoteDMATransfer(dst_ids=[dest(d, core, topo)], dma_engine_mask=m,
-                                                   remote_sem=sem.hc if what == 0 else sem.hp, src=src, dst=dst, alu_op=0))
+            for move in step:
+                if move[0] == "d":
+                    k = move[1]
+                    d, arrived = to[k], sem["x%d" % k]
+                    m = topo.mask(core, d)
+                    src, dst = both(T.xq, T.xs, 0, NC), both(T.rq, T.rs, NC * (k - 1), NC * k)
+                else:
+                    d = hs[move[1]]
+                    m = inner_mask(rank, d, T, topo)
+                    if move[0] == "x":
+                        src, arrived = both(T.xq, T.xs, 0, NC), (sem.hxc, sem.hxs)[what]
+                    else:
+                        p = move[2]
+                        src, arrived = both(T.wq, T.ws, *PIECES[p]), sem[("hwc%d", "hws%d")[what] % p]
+                        if what == 0:
+                            g.wait_ge(sem.wd, (PIECES[p][1] + 255) // 256)
+                    dst = src
+                transfers.append(RemoteDMATransfer(dst_ids=[dest(d, core, topo)], dma_engine_mask=m, remote_sem=arrived,
+                                                   src=src[what], dst=dst[what], alu_op=0))
                 sent += count(m)
             g.remote_dma_fused(transfers, local_sem=sem.sent)
-    for k in range(1, N):
-        g.wait_ge(sem.yc, k)
+    for n, k in enumerate(ROUNDS):
+        g.wait_ge(sem.yc, n + 1)
         d = back[k]
         rid, pid = topo.addr(d, core)
         m = topo.mask(core, d)
@@ -112,86 +129,133 @@ def rank_program(g, core, T, topo):
         sent += count(m)
     g.wait_ge(sem.sent, sent)
 
-    for k in range(N):
-        if k == 0:
-            xq, xs = T.xq[:], T.xs[:]
-            g.tensor.wait_ge(sem.xd, 1)
-        else:
-            xq, xs = part(T.rq, k), part(T.rs, k)
-            src = back[k]
-            g.tensor.wait_ge(sem["x%d" % k], 2 * count(topo.mask(src, core)))
-        for i in range(4):
-            if k == 0 and i % 2 == 0:
-                g.tensor.wait_ge(sem.wd, i // 2 + 1)
-            g.tensor.matmul_mx(T.pz[:, 512 * i:512 * i + NC], T.w1q[:, 128 * i:128 * i + 128], T.w1s[:, 128 * i:128 * i + 128],
-                               xq, xs, True, True).then_inc(sem.zc, 1)
-        b = k % 2
-        if k == 0:
-            g.tensor.wait_ge(sem.wd, 3)
-        g.tensor.wait_ge(sem.hd, k + 1)
-        if k >= 3:
-            g.tensor.wait_ge(sem.yc, k - 2)
-        out = T.po[:, 0:NC] if k == 0 else T.py[:, 512 * b:512 * b + NC]
-        g.tensor.matmul_mx(out, T.w2q[:], T.w2s[:], T.hq[:, NC * b:NC * b + NC], T.hs[:, NC * b:NC * b + NC],
-                           True, True).then_inc(sem.my, 1)
+    last = N - 1
 
-    for k in range(N):
-        for i in (0, 2):
-            g.scalar.wait_ge(sem.zc, 4 * k + i + 1)
-            g.scalar.activation(T.h[:, i:4 * NC:4], T.pz[:, 512 * i:512 * i + NC], ActivationFunctionType.Relu,
-                                scale=SCALE).then_inc(sem.asc, 1)
-        if k:
-            b = k % 2
-            g.scalar.wait_ge(sem.my, k + 1)
-            g.scalar.activation(part(T.ys, k), T.py[:, 512 * b:512 * b + NC], ActivationFunctionType.Copy).then_inc(sem.yc, 1)
+    def first(n, i):
+        wq, ws, xq, xs = T.wq, T.ws, T.xq[:], T.xs[:]
+        if n == 0:
+            if i == 0:
+                g.tensor.wait_ge(sem.xd, 1)
+            if i % 2 == 0:
+                g.tensor.wait_ge(sem.wd, i // 2 + 1)
+        else:
+            if n == last:
+                wq, ws = T.vq, T.vs
+                for p, (lo, hi) in enumerate(PIECES):
+                    if lo == 128 * i:
+                        g.tensor.wait_ge(sem["v%d" % p], 2 * count(topo.mask(back[SHIFT], core)))
+            else:
+                k = ROUNDS[n - 1]
+                xq, xs = part(T.rq, k), part(T.rs, k)
+                if i == 0:
+                    g.tensor.wait_ge(sem["x%d" % k], 2 * count(topo.mask(back[k], core)))
+            g.tensor.wait_ge(sem.asc if i % 2 == 0 else sem.avc, 2 * (n - 1) + i // 2 + 1)
+        g.tensor.matmul_mx(T.pz[:, 512 * i:512 * i + NC], wq[:, 128 * i:128 * i + 128], ws[:, 128 * i:128 * i + 128],
+                           xq, xs, True, True).then_inc(sem.zc, 1)
+
+    for i in range(4):
+        first(0, i)
+    for n in range(N):
+        ahead = AHEAD[n] if n < last else 0
+        for i in range(ahead):
+            first(n + 1, i)
+        b = n % 2
+        if n == 0:
+            g.tensor.wait_ge(sem.wd, 3)
+        g.tensor.wait_ge(sem.hd, n + 1)
+        if 3 <= n < last:
+            g.tensor.wait_ge(sem.yc, n - 2)
+        out = T.po[:, 0:NC] if n in (0, last) else T.py[:, 512 * b:512 * b + NC]
+        wq, ws = (T.vq, T.vs) if n == last else (T.wq, T.ws)
+        g.tensor.matmul_mx(out, wq[:, 512:WC], ws[:, 512:WC], T.hq[:, NC * b:NC * b + NC], T.hs[:, NC * b:NC * b + NC],
+                           n != last, n != 0).then_inc(sem.my, 1)
+        if n < last:
+            for i in range(ahead, 4):
+                first(n + 1, i)
+
+    def copy_out(n):
+        b = n % 2
+        g.scalar.wait_ge(sem.my, n + 1)
+        g.scalar.activation(part(T.ys, ROUNDS[n - 1]), T.py[:, 512 * b:512 * b + NC],
+                            ActivationFunctionType.Copy).then_inc(sem.yc, 1)
+
+    def act(n, i):
+        b = 4 * NC * (n % 2)
+        g.scalar.wait_ge(sem.zc, 4 * n + i + 1)
+        g.scalar.activation(T.h[:, b + i:b + 4 * NC:4], T.pz[:, 512 * i:512 * i + NC], ActivationFunctionType.Relu,
+                            scale=SCALE).then_inc(sem.asc, 1)
+
+    for n in range(N):
+        before = n > 1 and AHEAD[n - 1] == 0
+        if before:
+            copy_out(n - 1)
+        act(n, 0)
+        act(n, 2)
+        if n > 1 and not before:
+            copy_out(n - 1)
 
     g.vector.wait_ge(sem.ldx, 16)
     g.vector.quantize_mx(T.xq[:], T.xs[:], T.xb[:]).then_inc(sem.xd, 1)
     g.vector.wait_ge(sem.ldw1a, 16)
-    g.vector.quantize_mx(T.w1q[:, 0:256], T.w1s[:, 0:256], T.w1b[:, 0:1024]).then_inc(sem.wd, 1)
+    g.vector.quantize_mx(T.wq[:, 0:256], T.ws[:, 0:256], T.w1b[:, 0:1024]).then_inc(sem.wd, 1)
     g.vector.wait_ge(sem.ldw1b, 16)
-    g.vector.quantize_mx(T.w1q[:, 256:512], T.w1s[:, 256:512], T.w1b[:, 1024:2048]).then_inc(sem.wd, 1)
-    for k in range(N):
-        b = k % 2
+    g.vector.quantize_mx(T.wq[:, 256:512], T.ws[:, 256:512], T.w1b[:, 1024:2048]).then_inc(sem.wd, 1)
+    g.vector.wait_ge(sem.ldw2, 16)
+    g.vector.quantize_mx(T.wq[:, 512:WC], T.ws[:, 512:WC], T.w2b[:]).then_inc(sem.wd, 1)
+    for n in range(N):
+        b = n % 2
         for i in (1, 3):
-            g.vector.wait_ge(sem.zc, 4 * k + i + 1)
-            g.vector.tensor_scalar(T.h[:, i:4 * NC:4], T.pz[:, 512 * i:512 * i + NC], 0.0, SCALE,
+            g.vector.wait_ge(sem.zc, 4 * n + i + 1)
+            g.vector.tensor_scalar(T.h[:, 4 * NC * b + i:4 * NC * (b + 1):4], T.pz[:, 512 * i:512 * i + NC], 0.0, SCALE,
                                    AluOpType.max, AluOpType.mult).then_inc(sem.avc, 1)
-        g.vector.wait_ge(sem.asc, 2 * k + 2)
-        g.vector.wait_ge(sem.avc, 2 * k + 2)
-        g.vector.quantize_mx(T.hq[:, NC * b:NC * b + NC], T.hs[:, NC * b:NC * b + NC], T.h[:]).then_inc(sem.hd, 1)
-        if k == 0:
-            g.vector.wait_ge(sem.ldw2, 16)
-            g.vector.quantize_mx(T.w2q[:], T.w2s[:], T.w2b[:]).then_inc(sem.wd, 1)
-    g.vector.wait_ge(sem.my, 1)
-    for k in range(1, N):
-        src = to[k]
-        g.vector.wait_ge(sem["y%d" % k], count(topo.mask(src, core)))
-        if k > 1:
-            g.vector.wait_ge(sem.ad, k - 1)
-        g.vector.tensor_tensor(T.acc[:], T.po[:, 0:NC] if k == 1 else T.acc[:], part(T.yl, k),
-                               AluOpType.add).then_inc(sem.ad, 1)
+        g.vector.wait_ge(sem.asc, 2 * n + 2)
+        g.vector.wait_ge(sem.avc, 2 * n + 2)
+        if n >= 2:
+            g.vector.wait_ge(sem.my, n - 1)
+        g.vector.quantize_mx(T.hq[:, NC * b:NC * b + NC], T.hs[:, NC * b:NC * b + NC],
+                             T.h[:, 4 * NC * b:4 * NC * (b + 1)]).then_inc(sem.hd, 1)
 
-    g.sync.wait_ge(sem.ad, N - 1)
+    def landed(k):
+        g.vector.wait_ge(sem["y%d" % k], count(topo.mask(to[k], core)))
+        return part(T.yl, k)
+
+    terms = ROUNDS[:-1] + [0] + ROUNDS[-1:]
+    acc = landed(terms[0])
+    for n, k in enumerate(terms[1:]):
+        if k == 0:
+            g.vector.wait_ge(sem.my, N)
+            term = T.po[:, 0:NC]
+        else:
+            term = landed(k)
+        if n:
+            g.vector.wait_ge(sem.ad, n)
+        g.vector.tensor_tensor(T.acc[:], acc, term, AluOpType.add).then_inc(sem.ad, 1)
+        acc = T.acc[:]
+
+    g.sync.wait_ge(sem.ad, len(terms) - 1)
     g.sync.dma_start(T.y[:], T.acc[:]).then_inc(sem.st, 16)
     g.sync.wait_ge(sem.st, 16)
 
 
-def helper(g, core, rank, rounds, T, topo):
+def helper(g, core, rank, sends, T, topo):
     sem = T.sem
-    inner = count(topo.mask(T.cores[rank], core) & ~topo.mask(T.cores[rank], T.cores[(rank + 1) % N]))
-    sent = 0
-    for n, k in enumerate(rounds):
+    inner = count(inner_mask(rank, core, T, topo))
+    sent, seen = 0, []
+    for kind, i in sends:
+        if kind == "w":
+            k, arrived, came = SHIFT, sem["v%d" % i], (sem["hwc%d" % i], sem["hws%d" % i])
+            src, dst = both(T.wq, T.ws, *PIECES[i]), both(T.vq, T.vs, *PIECES[i])
+        else:
+            k, arrived, came = i, sem["x%d" % i], (sem.hxc, sem.hxs)
+            src, dst = both(T.xq, T.xs, 0, NC), both(T.rq, T.rs, NC * (k - 1), NC * k)
         d = T.cores[(rank + k) % N]
         rid, pid = topo.addr(d, core)
         m = topo.mask(core, d)
-        if n == 0:
-            g.wait_ge(sem.hc, inner)
-        g.remote_dma(out_ap=part(T.rq, k).bitcast(dt.uint8), in_ap=T.xq[:].bitcast(dt.uint8), remote_sem=sem["x%d" % k],
-                     local_sem=sem.sent, pid=pid, routing_id=rid, dma_engine_mask=m)
-        if n == 0:
-            g.wait_ge(sem.hp, inner)
-        g.remote_dma(out_ap=part(T.rs, k), in_ap=T.xs[:], remote_sem=sem["x%d" % k],
-                     local_sem=sem.sent, pid=pid, routing_id=rid, dma_engine_mask=m)
-        sent += 2 * count(m)
+        for what in range(2):
+            if kind == "w" or kind not in seen:
+                g.wait_ge(came[what], inner)
+            g.remote_dma(out_ap=dst[what], in_ap=src[what], remote_sem=arrived, local_sem=sem.sent, pid=pid, routing_id=rid,
+                         dma_engine_mask=m)
+            sent += count(m)
+        seen.append(kind)
     g.wait_ge(sem.sent, sent)

from concourse.bass import DstId, RemoteDMATransfer
from concourse.mybir import dt, AluOpType, ActivationFunctionType

N, NC, WC, SIM_CORES = 6, 192, 640, 256
SCALE = 0.019
SHIFT = 3
ROUNDS = [1, 2, 4, 5]
PIECES = [(0, 256), (256, WC)]
STEPS = [[("d", 1), ("x", 0)], [("d", 2)], [("w", 1, 0)], [("d", 4)], [("w", 0, 1)]]
VIA = [[("x", 5), ("w", 1)], [("w", 0)]]
AHEAD = [0, 0, 0, 3, 0]

SCRATCH = {
    "xb": ("sbuf", [128, 4 * NC], "bfloat16"),
    "w1b": ("sbuf", [128, 2048], "bfloat16"),
    "w2b": ("sbuf", [128, 512], "bfloat16"),
    "xq": ("sbuf", [128, NC], "float8_e4m3fn_x4"),
    "xs": ("sbuf", [128, NC], "uint8"),
    "wq": ("sbuf", [128, WC], "float8_e4m3fn_x4"),
    "ws": ("sbuf", [128, WC], "uint8"),
    "vq": ("sbuf", [128, WC], "float8_e4m3fn_x4"),
    "vs": ("sbuf", [128, WC], "uint8"),
    "rq": ("sbuf", [128, NC * (N - 1)], "float8_e4m3fn_x4"),
    "rs": ("sbuf", [128, NC * (N - 1)], "uint8"),
    "h": ("sbuf", [128, 8 * NC], "bfloat16"),
    "hq": ("sbuf", [128, 2 * NC], "float8_e4m3fn_x4"),
    "hs": ("sbuf", [128, 2 * NC], "uint8"),
    "ys": ("sbuf", [128, NC * (N - 1)], "float32"),
    "yl": ("sbuf", [128, NC * (N - 1)], "float32"),
    "acc": ("sbuf", [128, NC], "float32"),
    "pz": ("psum", [128, 2048], "float32"),
    "po": ("psum", [128, 512], "float32"),
    "py": ("psum", [128, 1024], "float32"),
}
SEMAPHORES = (["ldx", "ldw1a", "ldw1b", "ldw2", "xd", "wd", "zc", "asc", "avc", "hd", "my", "yc", "ad", "st", "sent", "hxc", "hxs"]
              + [s + "%d" % p for s in ("hwc", "hws", "v") for p in range(len(PIECES))]
              + [s + "%d" % k for s in ("x", "y") for k in range(1, N)])


def count(mask):
    return bin(mask).count("1")


def same_chip(topo, a, b):
    return topo.host(a) == topo.host(b) and topo.chip(a) == topo.chip(b)


def helpers_of(rank, T, topo):
    home = T.cores[rank]
    found = []
    for c in range(SIM_CORES):
        if same_chip(topo, c, home) and topo.die(c) != topo.die(home):
            if all(topo.may_write(c, d) for d in T.cores if d != home):
                found.append(c)
    return found[:len(VIA)]


def dest(d, src, topo):
    rid, pid = topo.addr(d, src)
    return DstId(rid=rid, pnc=pid)


def inner_mask(rank, h, T, topo):
    home = T.cores[rank]
    return topo.mask(home, h) & ~topo.mask(home, T.cores[(rank + 1) % N])


def part(buf, k):
    return buf[:, NC * (k - 1):NC * k]


def both(codes, planes, lo, hi):
    return codes[:, lo:hi].bitcast(dt.uint8), planes[:, lo:hi]


def rank_program(g, core, T, topo):
    rank = T.rank_of(core)
    if rank is None:
        for r in range(N):
            if same_chip(topo, core, T.cores[r]):
                hs = helpers_of(r, T, topo)
                if core in hs:
                    helper(g, core, r, VIA[hs.index(core)], T, topo)
        return

    sem = T.sem
    to = {k: T.cores[(rank + k) % N] for k in range(1, N)}
    back = {k: T.cores[(rank - k) % N] for k in range(1, N)}
    hs = helpers_of(rank, T, topo)

    g.sync.dma_start(T.xb[:], T.x[:]).then_inc(sem.ldx, 16)
    g.sync.dma_start(T.w1b[:, 0:1024], T.w1[:, 0:1024]).then_inc(sem.ldw1a, 16)
    g.sync.dma_start(T.w1b[:, 1024:2048], T.w1[:, 1024:2048]).then_inc(sem.ldw1b, 16)
    g.sync.dma_start(T.w2b[:], T.w2[:]).then_inc(sem.ldw2, 16)

    sent = 0
    g.wait_ge(sem.xd, 1)
    for step in STEPS:
        for what in range(2):
            transfers = []
            for move in step:
                if move[0] == "d":
                    k = move[1]
                    d, arrived = to[k], sem["x%d" % k]
                    m = topo.mask(core, d)
                    src, dst = both(T.xq, T.xs, 0, NC), both(T.rq, T.rs, NC * (k - 1), NC * k)
                else:
                    d = hs[move[1]]
                    m = inner_mask(rank, d, T, topo)
                    if move[0] == "x":
                        src, arrived = both(T.xq, T.xs, 0, NC), (sem.hxc, sem.hxs)[what]
                    else:
                        p = move[2]
                        src, arrived = both(T.wq, T.ws, *PIECES[p]), sem[("hwc%d", "hws%d")[what] % p]
                        if what == 0:
                            g.wait_ge(sem.wd, (PIECES[p][1] + 255) // 256)
                    dst = src
                transfers.append(RemoteDMATransfer(dst_ids=[dest(d, core, topo)], dma_engine_mask=m, remote_sem=arrived,
                                                   src=src[what], dst=dst[what], alu_op=0))
                sent += count(m)
            g.remote_dma_fused(transfers, local_sem=sem.sent)
    for n, k in enumerate(ROUNDS):
        g.wait_ge(sem.yc, n + 1)
        d = back[k]
        rid, pid = topo.addr(d, core)
        m = topo.mask(core, d)
        g.remote_dma(out_ap=part(T.yl, k), in_ap=part(T.ys, k), remote_sem=sem["y%d" % k], local_sem=sem.sent,
                     pid=pid, routing_id=rid, dma_engine_mask=m)
        sent += count(m)
    g.wait_ge(sem.sent, sent)

    last = N - 1

    def first(n, i):
        wq, ws, xq, xs = T.wq, T.ws, T.xq[:], T.xs[:]
        if n == 0:
            if i == 0:
                g.tensor.wait_ge(sem.xd, 1)
            if i % 2 == 0:
                g.tensor.wait_ge(sem.wd, i // 2 + 1)
        else:
            if n == last:
                wq, ws = T.vq, T.vs
                for p, (lo, hi) in enumerate(PIECES):
                    if lo == 128 * i:
                        g.tensor.wait_ge(sem["v%d" % p], 2 * count(topo.mask(back[SHIFT], core)))
            else:
                k = ROUNDS[n - 1]
                xq, xs = part(T.rq, k), part(T.rs, k)
                if i == 0:
                    g.tensor.wait_ge(sem["x%d" % k], 2 * count(topo.mask(back[k], core)))
            g.tensor.wait_ge(sem.asc if i % 2 == 0 else sem.avc, 2 * (n - 1) + i // 2 + 1)
        g.tensor.matmul_mx(T.pz[:, 512 * i:512 * i + NC], wq[:, 128 * i:128 * i + 128], ws[:, 128 * i:128 * i + 128],
                           xq, xs, True, True).then_inc(sem.zc, 1)

    for i in range(4):
        first(0, i)
    for n in range(N):
        ahead = AHEAD[n] if n < last else 0
        for i in range(ahead):
            first(n + 1, i)
        b = n % 2
        if n == 0:
            g.tensor.wait_ge(sem.wd, 3)
        g.tensor.wait_ge(sem.hd, n + 1)
        if 3 <= n < last:
            g.tensor.wait_ge(sem.yc, n - 2)
        out = T.po[:, 0:NC] if n in (0, last) else T.py[:, 512 * b:512 * b + NC]
        wq, ws = (T.vq, T.vs) if n == last else (T.wq, T.ws)
        g.tensor.matmul_mx(out, wq[:, 512:WC], ws[:, 512:WC], T.hq[:, NC * b:NC * b + NC], T.hs[:, NC * b:NC * b + NC],
                           n != last, n != 0).then_inc(sem.my, 1)
        if n < last:
            for i in range(ahead, 4):
                first(n + 1, i)

    def copy_out(n):
        b = n % 2
        g.scalar.wait_ge(sem.my, n + 1)
        g.scalar.activation(part(T.ys, ROUNDS[n - 1]), T.py[:, 512 * b:512 * b + NC],
                            ActivationFunctionType.Copy).then_inc(sem.yc, 1)

    def act(n, i):
        b = 4 * NC * (n % 2)
        g.scalar.wait_ge(sem.zc, 4 * n + i + 1)
        g.scalar.activation(T.h[:, b + i:b + 4 * NC:4], T.pz[:, 512 * i:512 * i + NC], ActivationFunctionType.Relu,
                            scale=SCALE).then_inc(sem.asc, 1)

    for n in range(N):
        before = n > 1 and AHEAD[n - 1] == 0
        if before:
            copy_out(n - 1)
        act(n, 0)
        act(n, 2)
        if n > 1 and not before:
            copy_out(n - 1)

    g.vector.wait_ge(sem.ldx, 16)
    g.vector.quantize_mx(T.xq[:], T.xs[:], T.xb[:]).then_inc(sem.xd, 1)
    g.vector.wait_ge(sem.ldw1a, 16)
    g.vector.quantize_mx(T.wq[:, 0:256], T.ws[:, 0:256], T.w1b[:, 0:1024]).then_inc(sem.wd, 1)
    g.vector.wait_ge(sem.ldw1b, 16)
    g.vector.quantize_mx(T.wq[:, 256:512], T.ws[:, 256:512], T.w1b[:, 1024:2048]).then_inc(sem.wd, 1)
    g.vector.wait_ge(sem.ldw2, 16)
    g.vector.quantize_mx(T.wq[:, 512:WC], T.ws[:, 512:WC], T.w2b[:]).then_inc(sem.wd, 1)
    for n in range(N):
        b = n % 2
        for i in (1, 3):
            g.vector.wait_ge(sem.zc, 4 * n + i + 1)
            g.vector.tensor_scalar(T.h[:, 4 * NC * b + i:4 * NC * (b + 1):4], T.pz[:, 512 * i:512 * i + NC], 0.0, SCALE,
                                   AluOpType.max, AluOpType.mult).then_inc(sem.avc, 1)
        g.vector.wait_ge(sem.asc, 2 * n + 2)
        g.vector.wait_ge(sem.avc, 2 * n + 2)
        if n >= 2:
            g.vector.wait_ge(sem.my, n - 1)
        g.vector.quantize_mx(T.hq[:, NC * b:NC * b + NC], T.hs[:, NC * b:NC * b + NC],
                             T.h[:, 4 * NC * b:4 * NC * (b + 1)]).then_inc(sem.hd, 1)

    def landed(k):
        g.vector.wait_ge(sem["y%d" % k], count(topo.mask(to[k], core)))
        return part(T.yl, k)

    terms = ROUNDS[:-1] + [0] + ROUNDS[-1:]
    acc = landed(terms[0])
    for n, k in enumerate(terms[1:]):
        if k == 0:
            g.vector.wait_ge(sem.my, N)
            term = T.po[:, 0:NC]
        else:
            term = landed(k)
        if n:
            g.vector.wait_ge(sem.ad, n)
        g.vector.tensor_tensor(T.acc[:], acc, term, AluOpType.add).then_inc(sem.ad, 1)
        acc = T.acc[:]

    g.sync.wait_ge(sem.ad, len(terms) - 1)
    g.sync.dma_start(T.y[:], T.acc[:]).then_inc(sem.st, 16)
    g.sync.wait_ge(sem.st, 16)


def helper(g, core, rank, sends, T, topo):
    sem = T.sem
    inner = count(inner_mask(rank, core, T, topo))
    sent, seen = 0, []
    for kind, i in sends:
        if kind == "w":
            k, arrived, came = SHIFT, sem["v%d" % i], (sem["hwc%d" % i], sem["hws%d" % i])
            src, dst = both(T.wq, T.ws, *PIECES[i]), both(T.vq, T.vs, *PIECES[i])
        else:
            k, arrived, came = i, sem["x%d" % i], (sem.hxc, sem.hxs)
            src, dst = both(T.xq, T.xs, 0, NC), both(T.rq, T.rs, NC * (k - 1), NC * k)
        d = T.cores[(rank + k) % N]
        rid, pid = topo.addr(d, core)
        m = topo.mask(core, d)
        for what in range(2):
            if kind == "w" or kind not in seen:
                g.wait_ge(came[what], inner)
            g.remote_dma(out_ap=dst[what], in_ap=src[what], remote_sem=arrived, local_sem=sem.sent, pid=pid, routing_id=rid,
                         dma_engine_mask=m)
            sent += count(m)
        seen.append(kind)
    g.wait_ge(sem.sent, sent)
